import numpy as np
import ml_dtypes


def mxq(x, axis, fmt="e4m3"):
    dtype, down = {"e4m3": (ml_dtypes.float8_e4m3fn, 7), "e5m2": (ml_dtypes.float8_e5m2, 14)}[fmt]
    v = np.moveaxis(np.asarray(x, np.float32).astype(ml_dtypes.bfloat16).astype(np.float64), axis, -1)
    blocks = v.reshape(v.shape[:-1] + (-1, 32))
    amax = np.abs(blocks).max(-1, keepdims=True)
    byte = np.maximum(np.where(amax > 0, np.frexp(amax)[1] - 1 + 127, 0) - down, 1)
    scale = np.exp2(byte - 127.0)
    codes = (blocks / scale).astype(np.float32).astype(dtype).astype(np.float64)
    return np.moveaxis((codes * scale).reshape(v.shape), -1, axis)


WIDE = False


def mx_kscale(k):
    if not WIDE:
        return np.ones(k)
    levels = np.array([10, -10, 5, -5, 0])
    if k % 512:
        return np.exp2(np.random.permutation(np.resize(levels, k // 32))).repeat(32)
    a = np.empty((k // 512, 16))
    for p in range(k // 512):
        a[p, :8] = np.random.permutation(np.resize(levels, 8))
        for g in range(8):
            far = levels[np.abs(levels - a[p, g]) >= 10]
            a[p, g + 8] = far[np.random.randint(len(far))]
    return np.exp2(a.ravel()).repeat(32)


def f64(x):
    return np.asarray(x).astype(np.float64)


def striped(idx):
    return np.tile(idx.reshape(-1, 16).T, (8, 1)).astype(np.uint16)


def unstriped(offs):
    return offs[:16].T.reshape(-1).astype(np.int64)


def striped8(idx):
    return np.concatenate([x.reshape(-1, 16).T for x in idx]).astype(np.uint16)


def runs(offs, k):
    lists = np.stack([offs[16 * r : 16 * r + 16].T.reshape(-1) for r in range(8)]).astype(np.int64)
    return lists[np.arange(k) % 512 // 64]


def pack_weight(w):
    k, n = w.shape
    w = f64(np.asarray(w, np.float32).astype(ml_dtypes.bfloat16)).reshape(k // 32, 32, n)
    amax = np.abs(w).max(1)
    byte = np.clip(np.where(amax > 0, np.frexp(amax)[1] - 1 + 127 - 7, 1), 1, 254)
    scaled = (w * np.exp2(127.0 - byte)[:, None, :]).reshape(k, n).astype(np.float32)
    words = np.ascontiguousarray(scaled.reshape(k // 512, 128, 4, n).transpose(0, 1, 3, 2)).astype(ml_dtypes.float8_e4m3fn).view(np.uint8)
    return words, np.ascontiguousarray(byte.astype(np.uint8).reshape(k // 512, 16, n))


def unpack_weight(words, scales):
    g, p, n, _ = words.shape
    vals = np.ascontiguousarray(words).view(ml_dtypes.float8_e4m3fn).astype(np.float64) * np.repeat(np.exp2(scales.astype(np.float64) - 127.0), 8, axis=1)[..., None]
    return vals.transpose(0, 1, 3, 2).reshape(g * 512, n)


def sigmoid(v):
    return 1.0 / (1.0 + np.exp(-np.maximum(v, -700.0)))


K, T, S, H, C, U = 512, 2048, 512, 512, 512, 1024


def setup_inputs():
    n = np.random.standard_normal
    s = mx_kscale(K)[:, None]
    packed_xT = pack_weight(n((K, T)) * s)
    return {
        "x_words": packed_xT[0],
        "x_scales": packed_xT[1],
        "w1": (n((K, H)) / np.sqrt(K) / s).astype(np.float32),
        "w2": (n((K, H)) / np.sqrt(K) / s).astype(np.float32),
        "gs": (np.random.uniform(0.5, 1.5, (K, 1)) / s).astype(np.float32),
        "mem": n((C, U)).astype(np.float32),
        "offs": striped(np.random.permutation(T)[:S]),
        "two": striped(np.random.permutation(T)[:S]),
        "n1": striped8(np.stack([np.random.permutation(S) for _ in range(8)])),
        "n2": striped8(np.stack([np.random.permutation(S) for _ in range(8)])),
        "n3": striped8(np.stack([np.random.permutation(S) for _ in range(8)])),
        "n4": striped8(np.stack([np.random.permutation(S) for _ in range(8)])),
        "cand": striped(np.random.permutation(T)[:C]),
        "n5": striped8(np.stack([np.random.permutation(U)[:S] for _ in range(8)])),
    }


def reference(x_words, x_scales, w1, w2, gs, mem, offs, two, n1, n2, n3, n4, cand, n5):
    old = f64(mem)[np.arange(C)[:, None], runs(n5, C)]
    x_cand = unpack_weight(x_words, x_scales)[:, unstriped(cand)]
    xq = unpack_weight(x_words, x_scales)[:, unstriped(offs)]
    y = mxq(f64(w1), 0, "e4m3").T @ xq
    x_two = unpack_weight(x_words, x_scales)[:, unstriped(two)]
    d = mxq(f64(w2), 0, "e4m3").T @ x_two
    z = f64(gs) * (np.maximum(y[np.arange(H)[:, None], runs(n1, H)] + d[np.arange(H)[:, None], runs(n3, H)], y[np.arange(H)[:, None], runs(n2, H)] + d[np.arange(H)[:, None], runs(n4, H)]))
    s = 0.0625 * ((x_cand.T @ mxq(z, 0, "e4m3")))
    nw = old + sigmoid(s) * (s - old)
    out = f64(mem).copy()
    out[np.arange(C)[:, None], runs(n5, C)] = nw
    return out

@@ -1,0 +1,256 @@
+from contextlib import ExitStack
+
+import concourse.mybir as mybir
+
+F32 = mybir.dt.float32
+BF16 = mybir.dt.bfloat16
+I32 = mybir.dt.int32
+U32 = mybir.dt.uint32
+U16 = mybir.dt.uint16
+U8 = mybir.dt.uint8
+FP8X4 = mybir.dt.float8_e4m3fn_x4
+ALU = mybir.AluOpType
+ACT = mybir.ActivationFunctionType
+
+P = 128
+PACK = 4
+K, T, S, U = 512, 2048, 512, 1024
+HALF = S // 2
+LIST_COLS = S // 16
+FLOPS = 3 * 2 * 512 * 512 * 512
+
+
+def tile_picked_twcpathbpaget_none_p_kernel(
+    tc, x_words, x_scales, w1, w2, gs, mem, offs, two, n1, n2, n3, n4, cand, n5, out
+):
+    nc = tc.nc
+    with ExitStack() as ctx:
+        keep = ctx.enter_context(tc.tile_pool(name="keep", bufs=1))
+        psum = ctx.enter_context(tc.psum_pool(name="psum", bufs=1))
+
+        def load_list(src, name):
+            tile = keep.tile([P, LIST_COLS], U16, name=name)
+            nc.sync.dma_start(tile[:], src)
+            return tile
+
+        def tile_of(name, cols, dtype):
+            return keep.tile([P, cols], dtype, name=name, align_bytes=64)
+
+        table_scales = tile_of("table_scales", T, U8)
+        nc.vector.memset(table_scales[:].bitcast(I32), 0)
+        y_rows = [tile_of("y_rows%d" % t, 2 * S, F32) for t in range(PACK)]
+        d_rows = [tile_of("d_rows%d" % t, 2 * S, F32) for t in range(PACK)]
+        for t in range(PACK):
+            nc.vector.memset(y_rows[t][:, S:], 0.0)
+            nc.gpsimd.memset(d_rows[t][:, S:], 0.0)
+
+        offs_l = load_list(offs, "offs_l")
+        two_l = load_list(two, "two_l")
+        cand_l = load_list(cand, "cand_l")
+        for q in range(4):
+            nc.sync.dma_start(
+                table_scales[32 * q : 32 * q + 4, :].bitcast(I32),
+                x_scales[0, 4 * q : 4 * q + 4, :].bitcast(I32),
+            )
+        w1_raw = keep.tile([P, PACK, K], F32, name="w1_raw")
+        nc.sync.dma_start(w1_raw[:], w1.rearrange("(p j) c -> p j c", j=PACK))
+        table_words = tile_of("table_words", T, U32)
+        nc.sync.dma_start(
+            table_words[:].bitcast(I32), x_words[0].rearrange("p c r -> p (c r)").bitcast(I32)
+        )
+        w2_raw = keep.tile([P, PACK, K], F32, name="w2_raw")
+        nc.sync.dma_start(w2_raw[:], w2.rearrange("(p j) c -> p j c", j=PACK))
+        n1_l = load_list(n1, "n1_l")
+        n2_l = load_list(n2, "n2_l")
+        n3_l = load_list(n3, "n3_l")
+        n4_l = load_list(n4, "n4_l")
+        gain = keep.tile([P, PACK], F32, name="gain")
+        nc.sync.dma_start(gain[:], gs.rearrange("(p t) o -> p (t o)", t=PACK))
+        n5_l = load_list(n5, "n5_l")
+        mem_dealt = mem.rearrange("(p t) u -> t p u", t=PACK)
+        out_dealt = out.rearrange("(p t) u -> t p u", t=PACK)
+        page = [tile_of("page%d" % t, U, F32) for t in range(PACK)]
+        for t in range(PACK):
+            nc.sync.dma_start(page[t][:], mem_dealt[t])
+
+        def pick(table, offsets, name, dtype):
+            picked = tile_of(name, S, dtype)
+            nc.vector.tensor_copy(picked[:], table[:].indirect(offsets[:]))
+            return picked
+
+        def round_weights(raw, name):
+            rounded = tile_of(name, PACK * K, BF16)
+            nc.scalar.activation(
+                rounded[:].rearrange("p (t m j) -> p m t j", t=PACK, j=PACK),
+                raw[:].rearrange("p j (m t) -> p m t j", t=PACK),
+                ACT.Copy,
+            )
+            return rounded
+
+        def quantise(rounded, cols, name):
+            codes = tile_of(name + "_codes", cols, U32)
+            scales = tile_of(name + "_scales", cols, U8)
+            nc.vector.quantize_mx(out=codes[:].bitcast(FP8X4), scales=scales[:], in_=rounded[:])
+            return codes, scales
+
+        def product(bank, cols, stationary, t, moving):
+            acc = psum.tile([P, cols], F32, name="acc", tag="bank%d" % bank)
+            rows = slice(t * P, (t + 1) * P)
+            nc.tensor.matmul_mx(
+                out=acc[:],
+                lhsT=stationary[0][:, rows].bitcast(FP8X4),
+                lhsT_scale=stationary[1][:, rows],
+                rhs=moving[0][:].bitcast(FP8X4),
+                rhs_scale=moving[1][:],
+                start=True,
+                stop=True,
+            )
+            return acc
+
+        offs_scales = pick(table_scales, offs_l, "offs_scales", U8)
+        two_scales = pick(table_scales, two_l, "two_scales", U8)
+        cand_scales = pick(table_scales, cand_l, "cand_scales", U8)
+        w1_q = quantise(round_weights(w1_raw, "w1_bf16"), K, "w1")
+        offs_words = pick(table_words, offs_l, "offs_words", U32)
+        y_acc = [product(t, S, w1_q, t, (offs_words, offs_scales)) for t in range(PACK)]
+        nc.scalar.copy(y_rows[0][:, :S], y_acc[0][:])
+        nc.scalar.copy(y_rows[1][:, :S], y_acc[1][:])
+        w2_bf16 = round_weights(w2_raw, "w2_bf16")
+        nc.scalar.copy(y_rows[2][:, :S], y_acc[2][:])
+        nc.scalar.copy(y_rows[3][:, :S], y_acc[3][:])
+        two_words = pick(table_words, two_l, "two_words", U32)
+        cand_words = pick(table_words, cand_l, "cand_words", U32)
+        cand_scales_dealt = tile_of("cand_scales_dealt", S, U8)
+        nc.vector.tensor_copy(
+            cand_scales_dealt[:].rearrange("p (t m) -> p t m", t=PACK),
+            cand_scales[:].rearrange("p (m t) -> p t m", t=PACK),
+        )
+        cand_words_dealt = tile_of("cand_words_dealt", S, U32)
+        nc.vector.tensor_copy(
+            cand_words_dealt[:].rearrange("p (t m) -> p t m", t=PACK),
+            cand_words[:].rearrange("p (m t) -> p t m", t=PACK),
+        )
+        cand_q = (cand_words_dealt, cand_scales_dealt)
+
+        whole = (0, S)
+        first = (0, HALF)
+        second = (HALF, S)
+
+        def entries(lst, part):
+            return lst[:, part[0] // 16 : part[1] // 16]
+
+        held = {}
+
+        def fetch(name, t, part, lst):
+            got = tile_of("%s_%d_%d" % (name, t, part[0]), part[1] - part[0], F32)
+            nc.vector.tensor_copy(got[:], y_rows[t][:].indirect(entries(lst, part)))
+            held[(name, t, part)] = got
+
+        def fetch_add(name, other, t, part, lst):
+            got = tile_of("%s_%d_%d" % (name, t, part[0]), part[1] - part[0], F32)
+            nc.vector.tensor_tensor(
+                got[:], d_rows[t][:].indirect(entries(lst, part)), held[(other, t, part)][:], ALU.add
+            )
+            held[(name, t, part)] = got
+
+        z_bf16 = {h: keep.tile([P, HALF, PACK], BF16, name="z_bf16_%d" % h[0], align_bytes=64) for h in (first, second)}
+
+        def larger(t, part):
+            got = tile_of("m_%d_%d" % (t, part[0]), part[1] - part[0], F32)
+            nc.vector.tensor_tensor(got[:], held[("a", t, part)][:], held[("b", t, part)][:], ALU.max)
+            for h in (first, second):
+                if part[0] <= h[0] and h[1] <= part[1]:
+                    nc.scalar.activation(
+                        z_bf16[h][:, :, t],
+                        got[:, h[0] - part[0] : h[1] - part[0]],
+                        ACT.Copy,
+                        scale=gain[:, t : t + 1],
+                    )
+
+        def u1(t, part):
+            fetch("u1", t, part, n1_l)
+
+        def u2(t, part):
+            fetch("u2", t, part, n2_l)
+
+        def a(t, part):
+            fetch_add("a", "u1", t, part, n3_l)
+
+        def b(t, part):
+            fetch_add("b", "u2", t, part, n4_l)
+
+        keep_old = [tile_of("keep_old%d" % t, S, F32) for t in range(PACK)]
+        gated = [tile_of("gated%d" % t, S, F32) for t in range(PACK)]
+        kept = [tile_of("kept%d" % t, S, F32) for t in range(PACK)]
+
+        def score(part):
+            z_q = quantise(z_bf16[part][:].rearrange("p c t -> p (c t)"), HALF, "z%d" % part[0])
+            cols = slice(part[0], part[1])
+            accs = []
+            for t in range(PACK):
+                acc = product(t + (PACK if part == second else 0), HALF, cand_q, t, z_q)
+                accs.append(acc)
+                th = tile_of("th_%d_%d" % (t, part[0]), HALF, F32)
+                nc.scalar.activation(th[:], acc[:], ACT.Tanh, scale=0.03125)
+                nc.scalar.activation(keep_old[t][:, cols], th[:], ACT.Copy, scale=-0.5, bias=0.5)
+            return accs
+
+        def gate(accs, t, part):
+            nc.scalar.activation(gated[t][:, part[0] : part[1]], accs[t][:], ACT.Silu, scale=0.0625)
+
+        def fetch_old(t, part):
+            cols = slice(part[0], part[1])
+            nc.vector.tensor_tensor(
+                kept[t][:, cols], page[t][:].indirect(entries(n5_l, part)), keep_old[t][:, cols], ALU.mult
+            )
+
+        def put(t):
+            nc.vector.tensor_tensor(page[t][:].indirect(n5_l[:]), kept[t][:], gated[t][:], ALU.add)
+            nc.sync.dma_start(out_dealt[t], page[t][:])
+
+        u1(0, whole)
+        u2(0, whole)
+        w2_q = quantise(w2_bf16, K, "w2")
+        for t in range(PACK):
+            d_acc = product(PACK + t, S, w2_q, t, (two_words, two_scales))
+            nc.scalar.copy(d_rows[t][:, :S], d_acc[:])
+        u1(1, whole)
+        u2(1, whole)
+        u1(2, whole)
+        a(0, whole)
+        b(0, whole)
+        u2(2, whole)
+        larger(0, whole)
+        a(1, whole)
+        b(1, whole)
+        a(2, whole)
+        larger(1, whole)
+        b(2, whole)
+        u1(3, first)
+        larger(2, whole)
+        u2(3, first)
+        a(3, first)
+        b(3, first)
+        u1(3, second)
+        larger(3, first)
+        u2(3, second)
+        a(3, second)
+        accs_first = score(first)
+        b(3, second)
+        larger(3, second)
+        fetch_old(0, first)
+        fetch_old(1, first)
+        accs_second = score(second)
+        for t in range(PACK):
+            gate(accs_first, t, first)
+            gate(accs_second, t, second)
+        fetch_old(2, first)
+        fetch_old(3, first)
+        fetch_old(0, second)
+        fetch_old(1, second)
+        put(0)
+        fetch_old(2, second)
+        put(1)
+        fetch_old(3, second)
+        put(2)
+        put(3)

@@ -33,33 +33,42 @@ def tile_picked_twcpathbpaget_none_p_kernel(
             nc.sync.dma_start(tile[:], src)
             return tile
 
-        def tile_of(name, cols, dtype):
-            return keep.tile([P, cols], dtype, name=name, align_bytes=64)
+        def tile_of(name, cols, dtype, tag=""):
+            return keep.tile([P, cols], dtype, name=name, tag=tag or name, align_bytes=64)
 
         table_scales = tile_of("table_scales", T, U8)
         nc.vector.memset(table_scales[:].bitcast(I32), 0)
         y_rows = [tile_of("y_rows%d" % t, 2 * S, F32) for t in range(PACK)]
         d_rows = [tile_of("d_rows%d" % t, 2 * S, F32) for t in range(PACK)]
-        for t in range(PACK):
-            nc.vector.memset(y_rows[t][:, S:], 0.0)
-            nc.gpsimd.memset(d_rows[t][:, S:], 0.0)
+        warm_in = keep.tile([P, 1], F32, name="warm_in")
+        warm_out = keep.tile([P, 1], F32, name="warm_out")
+        nc.gpsimd.memset(warm_in[:], 0.0)
 
         offs_l = load_list(offs, "offs_l")
-        two_l = load_list(two, "two_l")
-        cand_l = load_list(cand, "cand_l")
         for q in range(4):
             nc.sync.dma_start(
                 table_scales[32 * q : 32 * q + 4, :].bitcast(I32),
                 x_scales[0, 4 * q : 4 * q + 4, :].bitcast(I32),
             )
-        w1_raw = keep.tile([P, PACK, K], F32, name="w1_raw")
-        nc.sync.dma_start(w1_raw[:], w1.rearrange("(p j) c -> p j c", j=PACK))
+        nc.scalar.activation(warm_out[:], warm_in[:], ACT.Silu)
+        two_l = load_list(two, "two_l")
+        cand_l = load_list(cand, "cand_l")
+
+        def load_weights(w, name):
+            halves = []
+            for h in range(2):
+                raw = keep.tile([P, PACK, K // 2], F32, name="%s_raw%d" % (name, h))
+                cols = slice(h * K // 2, (h + 1) * K // 2)
+                nc.sync.dma_start(raw[:], w.rearrange("(p j) c -> p j c", j=PACK)[:, :, cols])
+                halves.append(raw)
+            return halves
+
+        w1_raw = load_weights(w1, "w1")
         table_words = tile_of("table_words", T, U32)
         nc.sync.dma_start(
             table_words[:].bitcast(I32), x_words[0].rearrange("p c r -> p (c r)").bitcast(I32)
         )
-        w2_raw = keep.tile([P, PACK, K], F32, name="w2_raw")
-        nc.sync.dma_start(w2_raw[:], w2.rearrange("(p j) c -> p j c", j=PACK))
+        w2_raw = load_weights(w2, "w2")
         n1_l = load_list(n1, "n1_l")
         n2_l = load_list(n2, "n2_l")
         n3_l = load_list(n3, "n3_l")
@@ -73,22 +82,24 @@ def tile_picked_twcpathbpaget_none_p_kernel(
         for t in range(PACK):
             nc.sync.dma_start(page[t][:], mem_dealt[t])
 
-        def pick(table, offsets, name, dtype):
-            picked = tile_of(name, S, dtype)
+        def pick(table, offsets, name, dtype, tag=""):
+            picked = tile_of(name, S, dtype, tag)
             nc.vector.tensor_copy(picked[:], table[:].indirect(offsets[:]))
             return picked
 
-        def round_weights(raw, name):
-            rounded = tile_of(name, PACK * K, BF16)
-            nc.scalar.activation(
-                rounded[:].rearrange("p (t m j) -> p m t j", t=PACK, j=PACK),
-                raw[:].rearrange("p j (m t) -> p m t j", t=PACK),
-                ACT.Copy,
-            )
+        def round_weights(raw, name, tag=""):
+            rounded = tile_of(name, PACK * K, BF16, tag)
+            dealt = rounded[:].rearrange("p (t m j) -> p m t j", t=PACK, j=PACK)
+            for h in range(2):
+                nc.scalar.activation(
+                    dealt[:, h * P // 2 : (h + 1) * P // 2],
+                    raw[h][:].rearrange("p j (m t) -> p m t j", t=PACK),
+                    ACT.Copy,
+                )
             return rounded
 
-        def quantise(rounded, cols, name):
-            codes = tile_of(name + "_codes", cols, U32)
+        def quantise(rounded, cols, name, tag=""):
+            codes = tile_of(name + "_codes", cols, U32, tag)
             scales = tile_of(name + "_scales", cols, U8)
             nc.vector.quantize_mx(out=codes[:].bitcast(FP8X4), scales=scales[:], in_=rounded[:])
             return codes, scales
@@ -115,10 +126,10 @@ def tile_picked_twcpathbpaget_none_p_kernel(
         y_acc = [product(t, S, w1_q, t, (offs_words, offs_scales)) for t in range(PACK)]
         nc.scalar.copy(y_rows[0][:, :S], y_acc[0][:])
         nc.scalar.copy(y_rows[1][:, :S], y_acc[1][:])
-        w2_bf16 = round_weights(w2_raw, "w2_bf16")
+        w2_bf16 = round_weights(w2_raw, "w2_bf16", "offs_words")
         nc.scalar.copy(y_rows[2][:, :S], y_acc[2][:])
         nc.scalar.copy(y_rows[3][:, :S], y_acc[3][:])
-        two_words = pick(table_words, two_l, "two_words", U32)
+        two_words = pick(table_words, two_l, "two_words", U32, "w1_bf16")
         cand_words = pick(table_words, cand_l, "cand_words", U32)
         cand_scales_dealt = tile_of("cand_scales_dealt", S, U8)
         nc.vector.tensor_copy(
@@ -141,19 +152,19 @@ def tile_picked_twcpathbpaget_none_p_kernel(
 
         held = {}
 
-        def fetch(name, t, part, lst):
-            got = tile_of("%s_%d_%d" % (name, t, part[0]), part[1] - part[0], F32)
+        def fetch(name, t, part, lst, tag):
+            got = tile_of("%s_%d_%d" % (name, t, part[0]), part[1] - part[0], F32, tag)
             nc.vector.tensor_copy(got[:], y_rows[t][:].indirect(entries(lst, part)))
             held[(name, t, part)] = got
 
-        def fetch_add(name, other, t, part, lst):
-            got = tile_of("%s_%d_%d" % (name, t, part[0]), part[1] - part[0], F32)
+        def fetch_add(name, other, t, part, lst, tag):
+            got = tile_of("%s_%d_%d" % (name, t, part[0]), part[1] - part[0], F32, tag)
             nc.vector.tensor_tensor(
                 got[:], d_rows[t][:].indirect(entries(lst, part)), held[(other, t, part)][:], ALU.add
             )
             held[(name, t, part)] = got
 
-        z_bf16 = {h: keep.tile([P, HALF, PACK], BF16, name="z_bf16_%d" % h[0], align_bytes=64) for h in (first, second)}
+        z_bf16 = {h: tile_of("z_bf16_%d" % h[0], HALF * PACK, BF16) for h in (first, second)}
 
         def larger(t, part):
             got = tile_of("m_%d_%d" % (t, part[0]), part[1] - part[0], F32)
@@ -161,52 +172,75 @@ def tile_picked_twcpathbpaget_none_p_kernel(
             for h in (first, second):
                 if part[0] <= h[0] and h[1] <= part[1]:
                     nc.scalar.activation(
-                        z_bf16[h][:, :, t],
+                        z_bf16[h][:].rearrange("p (c t) -> p c t", t=PACK)[:, :, t],
                         got[:, h[0] - part[0] : h[1] - part[0]],
                         ACT.Copy,
                         scale=gain[:, t : t + 1],
                     )
 
-        def u1(t, part):
-            fetch("u1", t, part, n1_l)
+        def u1(t, part, tag=""):
+            fetch("u1", t, part, n1_l, tag)
 
-        def u2(t, part):
-            fetch("u2", t, part, n2_l)
+        def u2(t, part, tag=""):
+            fetch("u2", t, part, n2_l, tag)
 
-        def a(t, part):
-            fetch_add("a", "u1", t, part, n3_l)
+        def a(t, part, tag=""):
+            fetch_add("a", "u1", t, part, n3_l, tag)
 
-        def b(t, part):
-            fetch_add("b", "u2", t, part, n4_l)
+        def b(t, part, tag=""):
+            fetch_add("b", "u2", t, part, n4_l, tag)
 
-        keep_old = [tile_of("keep_old%d" % t, S, F32) for t in range(PACK)]
-        gated = [tile_of("gated%d" % t, S, F32) for t in range(PACK)]
-        kept = [tile_of("kept%d" % t, S, F32) for t in range(PACK)]
+        def gates(acc, t, part):
+            cols = part[1] - part[0]
+            th = tile_of("th_%d_%d" % (t, part[0]), cols, F32)
+            nc.scalar.activation(th[:], acc, ACT.Tanh, scale=0.03125)
+            keep_old = tile_of("keep_old_%d_%d" % (t, part[0]), cols, F32)
+            nc.scalar.activation(keep_old[:], th[:], ACT.Copy, scale=-0.5, bias=0.5)
+            held[("keep_old", t, part)] = keep_old
 
-        def score(part):
-            z_q = quantise(z_bf16[part][:].rearrange("p c t -> p (c t)"), HALF, "z%d" % part[0])
-            cols = slice(part[0], part[1])
-            accs = []
-            for t in range(PACK):
-                acc = product(t + (PACK if part == second else 0), HALF, cand_q, t, z_q)
-                accs.append(acc)
-                th = tile_of("th_%d_%d" % (t, part[0]), HALF, F32)
-                nc.scalar.activation(th[:], acc[:], ACT.Tanh, scale=0.03125)
-                nc.scalar.activation(keep_old[t][:, cols], th[:], ACT.Copy, scale=-0.5, bias=0.5)
-            return accs
+        def gated(acc, t, part):
+            got = tile_of("gated_%d_%d" % (t, part[0]), part[1] - part[0], F32)
+            nc.scalar.activation(got[:], acc, ACT.Silu, scale=0.0625)
+            held[("gated", t, part)] = got
 
-        def gate(accs, t, part):
-            nc.scalar.activation(gated[t][:, part[0] : part[1]], accs[t][:], ACT.Silu, scale=0.0625)
+        s_acc = {}
 
-        def fetch_old(t, part):
-            cols = slice(part[0], part[1])
-            nc.vector.tensor_tensor(
-                kept[t][:, cols], page[t][:].indirect(entries(n5_l, part)), keep_old[t][:, cols], ALU.mult
+        def score(t, part, z_q):
+            if t < 2 or part == first:
+                bank = t + (PACK if part == second else 0)
+                s_acc[(t, part)] = psum.tile([P, S], F32, name="acc", tag="bank%d" % bank)
+            else:
+                s_acc[(t, part)] = s_acc[(t, first)]
+            rows = slice(t * P, (t + 1) * P)
+            nc.tensor.matmul_mx(
+                out=s_acc[(t, part)][:, part[0] : part[1]],
+                lhsT=cand_q[0][:, rows].bitcast(FP8X4),
+                lhsT_scale=cand_q[1][:, rows],
+                rhs=z_q[0][:].bitcast(FP8X4),
+                rhs_scale=z_q[1][:],
+                start=True,
+                stop=True,
             )
 
-        def put(t):
-            nc.vector.tensor_tensor(page[t][:].indirect(n5_l[:]), kept[t][:], gated[t][:], ALU.add)
-            nc.sync.dma_start(out_dealt[t], page[t][:])
+        def acc_of(t, part):
+            return s_acc[(t, second if part == second else first)][:, part[0] : part[1]]
+
+        def fetch_old(t, part):
+            kept = tile_of("kept_%d_%d" % (t, part[0]), part[1] - part[0], F32)
+            nc.vector.tensor_tensor(
+                kept[:], page[t][:].indirect(entries(n5_l, part)), held[("keep_old", t, part)][:], ALU.mult
+            )
+            held[("kept", t, part)] = kept
+
+        def put(t, part):
+            nc.vector.tensor_tensor(
+                page[t][:].indirect(entries(n5_l, part)),
+                held[("kept", t, part)][:],
+                held[("gated", t, part)][:],
+                ALU.add,
+            )
+            if part[1] == S:
+                nc.sync.dma_start(out_dealt[t], page[t][:])
 
         u1(0, whole)
         u2(0, whole)
@@ -217,40 +251,52 @@ def tile_picked_twcpathbpaget_none_p_kernel(
         u1(1, whole)
         u2(1, whole)
         u1(2, whole)
+        u2(2, whole)
+        u1(3, first)
+        u2(3, first)
         a(0, whole)
         b(0, whole)
-        u2(2, whole)
-        larger(0, whole)
         a(1, whole)
+        larger(0, whole)
         b(1, whole)
         a(2, whole)
         larger(1, whole)
         b(2, whole)
-        u1(3, first)
-        larger(2, whole)
-        u2(3, first)
         a(3, first)
+        larger(2, whole)
         b(3, first)
-        u1(3, second)
+        u1(3, second, "u1_3_0")
         larger(3, first)
-        u2(3, second)
+        u2(3, second, "u2_3_0")
         a(3, second)
-        accs_first = score(first)
-        b(3, second)
+        z_first = quantise(z_bf16[first], HALF, "z_first")
+        for t in range(PACK):
+            score(t, first, z_first)
+        for t in range(2):
+            gates(acc_of(t, first), t, first)
+        b(3, second, "z_bf16_0")
         larger(3, second)
+        for t in range(2):
+            gated(acc_of(t, first), t, first)
         fetch_old(0, first)
         fetch_old(1, first)
-        accs_second = score(second)
+        put(0, first)
+        z_second = quantise(z_bf16[second], HALF, "z_second", "keep_old_1_0")
         for t in range(PACK):
-            gate(accs_first, t, first)
-            gate(accs_second, t, second)
-        fetch_old(2, first)
-        fetch_old(3, first)
+            score(t, second, z_second)
+        for t in range(2):
+            gates(acc_of(t, second), t, second)
+        for t in range(2):
+            gated(acc_of(t, second), t, second)
+        for t in range(2, PACK):
+            gates(acc_of(t, whole), t, whole)
+            gated(acc_of(t, whole), t, whole)
+        put(1, first)
         fetch_old(0, second)
         fetch_old(1, second)
-        put(0)
-        fetch_old(2, second)
-        put(1)
-        fetch_old(3, second)
-        put(2)
-        put(3)
+        put(0, second)
+        fetch_old(2, whole)
+        put(1, second)
+        fetch_old(3, whole)
+        put(2, whole)
+        put(3, whole)

@@ -16,6 +16,7 @@ P = 128
 PACK = 4
 K, T, S, U = 512, 2048, 512, 1024
 HALF = S // 2
+W1_SPLIT = 384
 LIST_COLS = S // 16
 FLOPS = 3 * 2 * 512 * 512 * 512
 
@@ -38,7 +39,6 @@ def tile_picked_twcpathbpaget_none_p_kernel(
 
         table_scales = tile_of("table_scales", T, U8)
         nc.vector.memset(table_scales[:].bitcast(I32), 0)
-        y_rows = [tile_of("y_rows%d" % t, 2 * S, F32) for t in range(PACK)]
         d_rows = [tile_of("d_rows%d" % t, 2 * S, F32) for t in range(PACK)]
         warm_in = keep.tile([P, 1], F32, name="warm_in")
         warm_out = keep.tile([P, 1], F32, name="warm_out")
@@ -54,21 +54,18 @@ def tile_picked_twcpathbpaget_none_p_kernel(
         two_l = load_list(two, "two_l")
         cand_l = load_list(cand, "cand_l")
 
-        def load_weights(w, name):
-            halves = []
-            for h in range(2):
-                raw = keep.tile([P, PACK, K // 2], F32, name="%s_raw%d" % (name, h))
-                cols = slice(h * K // 2, (h + 1) * K // 2)
-                nc.sync.dma_start(raw[:], w.rearrange("(p j) c -> p j c", j=PACK)[:, :, cols])
-                halves.append(raw)
-            return halves
+        def load_weights(w, name, cols):
+            raw = keep.tile([P, PACK, cols[1] - cols[0]], F32, name=name, align_bytes=64)
+            nc.sync.dma_start(raw[:], w.rearrange("(p j) c -> p j c", j=PACK)[:, :, cols[0] : cols[1]])
+            return raw, cols
 
-        w1_raw = load_weights(w1, "w1")
+        w1_raw = [load_weights(w1, "w1_raw0", (0, W1_SPLIT))]
         table_words = tile_of("table_words", T, U32)
         nc.sync.dma_start(
             table_words[:].bitcast(I32), x_words[0].rearrange("p c r -> p (c r)").bitcast(I32)
         )
-        w2_raw = load_weights(w2, "w2")
+        w1_raw.append(load_weights(w1, "w1_raw1", (W1_SPLIT, K)))
+        w2_raw = [load_weights(w2, "w2_raw0", (0, K // 2)), load_weights(w2, "w2_raw1", (K // 2, K))]
         n1_l = load_list(n1, "n1_l")
         n2_l = load_list(n2, "n2_l")
         n3_l = load_list(n3, "n3_l")
@@ -90,10 +87,10 @@ def tile_picked_twcpathbpaget_none_p_kernel(
         def round_weights(raw, name, tag=""):
             rounded = tile_of(name, PACK * K, BF16, tag)
             dealt = rounded[:].rearrange("p (t m j) -> p m t j", t=PACK, j=PACK)
-            for h in range(2):
+            for part, cols in raw:
                 nc.scalar.activation(
-                    dealt[:, h * P // 2 : (h + 1) * P // 2],
-                    raw[h][:].rearrange("p j (m t) -> p m t j", t=PACK),
+                    dealt[:, cols[0] // PACK : cols[1] // PACK],
+                    part[:].rearrange("p j (m t) -> p m t j", t=PACK),
                     ACT.Copy,
                 )
             return rounded
@@ -124,24 +121,24 @@ def tile_picked_twcpathbpaget_none_p_kernel(
         w1_q = quantise(round_weights(w1_raw, "w1_bf16"), K, "w1")
         offs_words = pick(table_words, offs_l, "offs_words", U32)
         y_acc = [product(t, S, w1_q, t, (offs_words, offs_scales)) for t in range(PACK)]
+        y_rows = [tile_of("y_rows%d" % t, 2 * S, F32) for t in range(2)]
         nc.scalar.copy(y_rows[0][:, :S], y_acc[0][:])
         nc.scalar.copy(y_rows[1][:, :S], y_acc[1][:])
-        w2_bf16 = round_weights(w2_raw, "w2_bf16", "offs_words")
+        w2_bf16 = round_weights(w2_raw, "w2_bf16")
+        y_rows.append(tile_of("y_rows2", 2 * S, F32, "w2_raw1"))
+        y_rows.append(tile_of("y_rows3", 2 * S, F32))
         nc.scalar.copy(y_rows[2][:, :S], y_acc[2][:])
         nc.scalar.copy(y_rows[3][:, :S], y_acc[3][:])
+        cand_words = pick(table_words, cand_l, "cand_words", U32, "w1_raw1")
         two_words = pick(table_words, two_l, "two_words", U32, "w1_bf16")
-        cand_words = pick(table_words, cand_l, "cand_words", U32)
-        cand_scales_dealt = tile_of("cand_scales_dealt", S, U8)
-        nc.vector.tensor_copy(
-            cand_scales_dealt[:].rearrange("p (t m) -> p t m", t=PACK),
-            cand_scales[:].rearrange("p (m t) -> p t m", t=PACK),
-        )
-        cand_words_dealt = tile_of("cand_words_dealt", S, U32)
-        nc.vector.tensor_copy(
-            cand_words_dealt[:].rearrange("p (t m) -> p t m", t=PACK),
-            cand_words[:].rearrange("p (m t) -> p t m", t=PACK),
-        )
-        cand_q = (cand_words_dealt, cand_scales_dealt)
+
+        def deal(picked, name, dtype, tag):
+            dealt = tile_of(name, S, dtype, tag)
+            nc.vector.tensor_copy(
+                dealt[:].rearrange("p (t m) -> p t m", t=PACK),
+                picked[:].rearrange("p (m t) -> p t m", t=PACK),
+            )
+            return dealt
 
         whole = (0, S)
         first = (0, HALF)
@@ -205,7 +202,7 @@ def tile_picked_twcpathbpaget_none_p_kernel(
 
         s_acc = {}
 
-        def score(t, part, z_q):
+        def score(t, part, cand_q, z_q):
             if t < 2 or part == first:
                 bank = t + (PACK if part == second else 0)
                 s_acc[(t, part)] = psum.tile([P, S], F32, name="acc", tag="bank%d" % bank)
@@ -244,12 +241,12 @@ def tile_picked_twcpathbpaget_none_p_kernel(
 
         u1(0, whole)
         u2(0, whole)
+        u1(1, whole)
+        u2(1, whole)
         w2_q = quantise(w2_bf16, K, "w2")
         for t in range(PACK):
             d_acc = product(PACK + t, S, w2_q, t, (two_words, two_scales))
             nc.scalar.copy(d_rows[t][:, :S], d_acc[:])
-        u1(1, whole)
-        u2(1, whole)
         u1(2, whole)
         u2(2, whole)
         u1(3, first)
@@ -268,35 +265,33 @@ def tile_picked_twcpathbpaget_none_p_kernel(
         u1(3, second, "u1_3_0")
         larger(3, first)
         u2(3, second, "u2_3_0")
-        a(3, second)
+        cand_q = (
+            deal(cand_words, "cand_words_dealt", U32, "a_2_0"),
+            deal(cand_scales, "cand_scales_dealt", U8, "b_2_0"),
+        )
         z_first = quantise(z_bf16[first], HALF, "z_first")
         for t in range(PACK):
-            score(t, first, z_first)
+            score(t, first, cand_q, z_first)
         for t in range(2):
             gates(acc_of(t, first), t, first)
-        b(3, second, "z_bf16_0")
+        a(3, second)
+        b(3, second)
         larger(3, second)
         for t in range(2):
             gated(acc_of(t, first), t, first)
         fetch_old(0, first)
         fetch_old(1, first)
+        z_second = quantise(z_bf16[second], HALF, "z_second", "keep_old_0_0")
         put(0, first)
-        z_second = quantise(z_bf16[second], HALF, "z_second", "keep_old_1_0")
-        for t in range(PACK):
-            score(t, second, z_second)
-        for t in range(2):
-            gates(acc_of(t, second), t, second)
-        for t in range(2):
-            gated(acc_of(t, second), t, second)
-        for t in range(2, PACK):
-            gates(acc_of(t, whole), t, whole)
-            gated(acc_of(t, whole), t, whole)
         put(1, first)
-        fetch_old(0, second)
-        fetch_old(1, second)
-        put(0, second)
-        fetch_old(2, whole)
-        put(1, second)
-        fetch_old(3, whole)
-        put(2, whole)
-        put(3, whole)
+        for t in range(PACK):
+            score(t, second, cand_q, z_second)
+        last = [second, second, whole, whole]
+        for t in range(PACK):
+            gates(acc_of(t, last[t]), t, last[t])
+        for t in range(PACK):
+            gated(acc_of(t, last[t]), t, last[t])
+        for t in range(PACK):
+            fetch_old(t, last[t])
+        for t in range(PACK):
+            put(t, last[t])

@@ -16,7 +16,7 @@ P = 128
 PACK = 4
 K, T, S, U = 512, 2048, 512, 1024
 HALF = S // 2
-W1_SPLIT = 384
+W1_SPLIT = 320
 LIST_COLS = S // 16
 FLOPS = 3 * 2 * 512 * 512 * 512
 
@@ -118,8 +118,10 @@ def tile_picked_twcpathbpaget_none_p_kernel(
         offs_scales = pick(table_scales, offs_l, "offs_scales", U8)
         two_scales = pick(table_scales, two_l, "two_scales", U8)
         cand_scales = pick(table_scales, cand_l, "cand_scales", U8)
-        w1_q = quantise(round_weights(w1_raw, "w1_bf16"), K, "w1")
         offs_words = pick(table_words, offs_l, "offs_words", U32)
+        cand_words = pick(table_words, cand_l, "cand_words", U32)
+        w1_q = quantise(round_weights(w1_raw, "w1_bf16"), K, "w1")
+        two_words = pick(table_words, two_l, "two_words", U32, "w1_raw1")
         y_acc = [product(t, S, w1_q, t, (offs_words, offs_scales)) for t in range(PACK)]
         y_rows = [tile_of("y_rows%d" % t, 2 * S, F32) for t in range(2)]
         nc.scalar.copy(y_rows[0][:, :S], y_acc[0][:])
@@ -129,8 +131,6 @@ def tile_picked_twcpathbpaget_none_p_kernel(
         y_rows.append(tile_of("y_rows3", 2 * S, F32))
         nc.scalar.copy(y_rows[2][:, :S], y_acc[2][:])
         nc.scalar.copy(y_rows[3][:, :S], y_acc[3][:])
-        cand_words = pick(table_words, cand_l, "cand_words", U32, "w1_raw1")
-        two_words = pick(table_words, two_l, "two_words", U32, "w1_bf16")
 
         def deal(picked, name, dtype, tag):
             dealt = tile_of(name, S, dtype, tag)
@@ -140,6 +140,7 @@ def tile_picked_twcpathbpaget_none_p_kernel(
             )
             return dealt
 
+        cand_scales_dealt = deal(cand_scales, "cand_scales_dealt", U8, "w1_bf16")
         whole = (0, S)
         first = (0, HALF)
         second = (HALF, S)
@@ -156,9 +157,11 @@ def tile_picked_twcpathbpaget_none_p_kernel(
 
         def fetch_add(name, other, t, part, lst, tag):
             got = tile_of("%s_%d_%d" % (name, t, part[0]), part[1] - part[0], F32, tag)
-            nc.vector.tensor_tensor(
-                got[:], d_rows[t][:].indirect(entries(lst, part)), held[(other, t, part)][:], ALU.add
-            )
+            if (other, t, part) in held:
+                addend = held[(other, t, part)][:]
+            else:
+                addend = held[(other, t, whole)][:, part[0] : part[1]]
+            nc.vector.tensor_tensor(got[:], d_rows[t][:].indirect(entries(lst, part)), addend, ALU.add)
             held[(name, t, part)] = got
 
         z_bf16 = {h: tile_of("z_bf16_%d" % h[0], HALF * PACK, BF16) for h in (first, second)}
@@ -187,53 +190,40 @@ def tile_picked_twcpathbpaget_none_p_kernel(
         def b(t, part, tag=""):
             fetch_add("b", "u2", t, part, n4_l, tag)
 
-        def gates(acc, t, part):
-            cols = part[1] - part[0]
-            th = tile_of("th_%d_%d" % (t, part[0]), cols, F32)
-            nc.scalar.activation(th[:], acc, ACT.Tanh, scale=0.03125)
-            keep_old = tile_of("keep_old_%d_%d" % (t, part[0]), cols, F32)
-            nc.scalar.activation(keep_old[:], th[:], ACT.Copy, scale=-0.5, bias=0.5)
-            held[("keep_old", t, part)] = keep_old
-
-        def gated(acc, t, part):
-            got = tile_of("gated_%d_%d" % (t, part[0]), part[1] - part[0], F32)
-            nc.scalar.activation(got[:], acc, ACT.Silu, scale=0.0625)
-            held[("gated", t, part)] = got
+        def piece(name, t, part, tag=""):
+            span = part if t < 2 else whole
+            if (name, t, span) not in held:
+                held[(name, t, span)] = tile_of("%s_%d_%d" % (name, t, span[0]), span[1] - span[0], F32, tag)
+            return held[(name, t, span)][:, part[0] - span[0] : part[1] - span[0]]
 
         s_acc = {}
 
         def score(t, part, cand_q, z_q):
-            if t < 2 or part == first:
-                bank = t + (PACK if part == second else 0)
-                s_acc[(t, part)] = psum.tile([P, S], F32, name="acc", tag="bank%d" % bank)
-            else:
-                s_acc[(t, part)] = s_acc[(t, first)]
-            rows = slice(t * P, (t + 1) * P)
-            nc.tensor.matmul_mx(
-                out=s_acc[(t, part)][:, part[0] : part[1]],
-                lhsT=cand_q[0][:, rows].bitcast(FP8X4),
-                lhsT_scale=cand_q[1][:, rows],
-                rhs=z_q[0][:].bitcast(FP8X4),
-                rhs_scale=z_q[1][:],
-                start=True,
-                stop=True,
-            )
+            bank = t + (PACK if part == second else 0)
+            acc = product(bank, HALF, cand_q, t, z_q)
+            s_acc[(t, part)] = acc
 
-        def acc_of(t, part):
-            return s_acc[(t, second if part == second else first)][:, part[0] : part[1]]
+        def gates(t, part):
+            th = tile_of("th_%d_%d" % (t, part[0]), HALF, F32)
+            nc.scalar.activation(th[:], s_acc[(t, part)][:], ACT.Tanh, scale=0.03125)
+            nc.scalar.activation(piece("keep_old", t, part), th[:], ACT.Copy, scale=-0.5, bias=0.5)
+
+        def gated(t, part, tag=""):
+            nc.scalar.activation(piece("gated", t, part, tag), s_acc[(t, part)][:], ACT.Silu, scale=0.0625)
 
         def fetch_old(t, part):
-            kept = tile_of("kept_%d_%d" % (t, part[0]), part[1] - part[0], F32)
             nc.vector.tensor_tensor(
-                kept[:], page[t][:].indirect(entries(n5_l, part)), held[("keep_old", t, part)][:], ALU.mult
+                piece("kept", t, part),
+                page[t][:].indirect(entries(n5_l, part)),
+                piece("keep_old", t, part),
+                ALU.mult,
             )
-            held[("kept", t, part)] = kept
 
         def put(t, part):
             nc.vector.tensor_tensor(
                 page[t][:].indirect(entries(n5_l, part)),
-                held[("kept", t, part)][:],
-                held[("gated", t, part)][:],
+                piece("kept", t, part),
+                piece("gated", t, part),
                 ALU.add,
             )
             if part[1] == S:
@@ -249,49 +239,56 @@ def tile_picked_twcpathbpaget_none_p_kernel(
             nc.scalar.copy(d_rows[t][:, :S], d_acc[:])
         u1(2, whole)
         u2(2, whole)
-        u1(3, first)
-        u2(3, first)
         a(0, whole)
         b(0, whole)
         a(1, whole)
         larger(0, whole)
         b(1, whole)
-        a(2, whole)
+        a(2, first)
         larger(1, whole)
-        b(2, whole)
+        b(2, first)
+        u1(3, first, "u1_1_0")
+        larger(2, first)
+        u2(3, first, "u2_1_0")
         a(3, first)
-        larger(2, whole)
         b(3, first)
-        u1(3, second, "u1_3_0")
+        u1(3, second, "u1_1_0")
         larger(3, first)
-        u2(3, second, "u2_3_0")
-        cand_q = (
-            deal(cand_words, "cand_words_dealt", U32, "a_2_0"),
-            deal(cand_scales, "cand_scales_dealt", U8, "b_2_0"),
-        )
+        u2(3, second, "u2_1_0")
+        cand_q = (deal(cand_words, "cand_words_dealt", U32, "a_1_0"), cand_scales_dealt)
+        a(2, second, "a_3_0")
         z_first = quantise(z_bf16[first], HALF, "z_first")
         for t in range(PACK):
             score(t, first, cand_q, z_first)
         for t in range(2):
-            gates(acc_of(t, first), t, first)
-        a(3, second)
-        b(3, second)
+            gates(t, first)
+        gated(0, first)
+        a(3, second, "b_3_0")
+        b(2, second, "z_bf16_0")
+        b(3, second, "m_3_0")
+        larger(2, second)
         larger(3, second)
-        for t in range(2):
-            gated(acc_of(t, first), t, first)
+        gated(1, first, "m_3_256")
+        for t in range(2, PACK):
+            gates(t, first)
         fetch_old(0, first)
         fetch_old(1, first)
-        z_second = quantise(z_bf16[second], HALF, "z_second", "keep_old_0_0")
         put(0, first)
+        z_second = quantise(z_bf16[second], HALF, "z_second", "keep_old_1_0")
         put(1, first)
+        fetch_old(2, first)
         for t in range(PACK):
             score(t, second, cand_q, z_second)
-        last = [second, second, whole, whole]
         for t in range(PACK):
-            gates(acc_of(t, last[t]), t, last[t])
+            gates(t, second)
         for t in range(PACK):
-            gated(acc_of(t, last[t]), t, last[t])
-        for t in range(PACK):
-            fetch_old(t, last[t])
-        for t in range(PACK):
-            put(t, last[t])
+            if t >= 2:
+                gated(t, first)
+            gated(t, second)
+        for t in range(PACK - 1):
+            fetch_old(t, second)
+        fetch_old(3, whole)
+        put(0, second)
+        put(1, second)
+        put(2, whole)
+        put(3, whole)

@@ -14,10 +14,15 @@ ACT = mybir.ActivationFunctionType
 
 P = 128
 PACK = 4
+GROUP = 16
+BLOCK = 32
+QUADRANT = 32
+SCALE_ROWS = QUADRANT * PACK // BLOCK
 K, T, S, U = 512, 2048, 512, 1024
 HALF = S // 2
+WHOLE, FIRST, SECOND = (0, S), (0, HALF), (HALF, S)
+SCORE_SCALE = 0.0625
 W1_SPLIT = 320
-LIST_COLS = S // 16
 FLOPS = 3 * 2 * 512 * 512 * 512
 
 
@@ -29,13 +34,18 @@ def tile_picked_twcpathbpaget_none_p_kernel(
         keep = ctx.enter_context(tc.tile_pool(name="keep", bufs=1))
         psum = ctx.enter_context(tc.psum_pool(name="psum", bufs=1))
 
-        def load_list(src, name):
-            tile = keep.tile([P, LIST_COLS], U16, name=name)
-            nc.sync.dma_start(tile[:], src)
-            return tile
+        def tile_of(name, cols, dtype, reuse=""):
+            return keep.tile([P, cols], dtype, name=name, tag=reuse or name, align_bytes=64)
 
-        def tile_of(name, cols, dtype, tag=""):
-            return keep.tile([P, cols], dtype, name=name, tag=tag or name, align_bytes=64)
+        def load_list(src, name):
+            offsets = keep.tile([P, S // GROUP], U16, name=name)
+            nc.sync.dma_start(offsets[:], src)
+            return offsets
+
+        def load_weights(w, name, cols):
+            raw = keep.tile([P, PACK, cols[1] - cols[0]], F32, name=name, align_bytes=64)
+            nc.sync.dma_start(raw[:], w.rearrange("(p j) c -> p j c", j=PACK)[:, :, cols[0] : cols[1]])
+            return raw, cols
 
         table_scales = tile_of("table_scales", T, U8)
         nc.vector.memset(table_scales[:].bitcast(I32), 0)
@@ -44,21 +54,15 @@ def tile_picked_twcpathbpaget_none_p_kernel(
         warm_out = keep.tile([P, 1], F32, name="warm_out")
         nc.gpsimd.memset(warm_in[:], 0.0)
 
-        offs_l = load_list(offs, "offs_l")
-        for q in range(4):
+        offs_list = load_list(offs, "offs_list")
+        for r in range(SCALE_ROWS):
             nc.sync.dma_start(
-                table_scales[32 * q : 32 * q + 4, :].bitcast(I32),
-                x_scales[0, 4 * q : 4 * q + 4, :].bitcast(I32),
+                table_scales[r:P:QUADRANT, :].bitcast(I32),
+                x_scales[0, r : K // BLOCK : SCALE_ROWS, :].bitcast(I32),
             )
         nc.scalar.activation(warm_out[:], warm_in[:], ACT.Silu)
-        two_l = load_list(two, "two_l")
-        cand_l = load_list(cand, "cand_l")
-
-        def load_weights(w, name, cols):
-            raw = keep.tile([P, PACK, cols[1] - cols[0]], F32, name=name, align_bytes=64)
-            nc.sync.dma_start(raw[:], w.rearrange("(p j) c -> p j c", j=PACK)[:, :, cols[0] : cols[1]])
-            return raw, cols
-
+        two_list = load_list(two, "two_list")
+        cand_list = load_list(cand, "cand_list")
         w1_raw = [load_weights(w1, "w1_raw0", (0, W1_SPLIT))]
         table_words = tile_of("table_words", T, U32)
         nc.sync.dma_start(
@@ -66,37 +70,37 @@ def tile_picked_twcpathbpaget_none_p_kernel(
         )
         w1_raw.append(load_weights(w1, "w1_raw1", (W1_SPLIT, K)))
         w2_raw = [load_weights(w2, "w2_raw0", (0, K // 2)), load_weights(w2, "w2_raw1", (K // 2, K))]
-        n1_l = load_list(n1, "n1_l")
-        n2_l = load_list(n2, "n2_l")
-        n3_l = load_list(n3, "n3_l")
-        n4_l = load_list(n4, "n4_l")
+        n1_list = load_list(n1, "n1_list")
+        n2_list = load_list(n2, "n2_list")
+        n3_list = load_list(n3, "n3_list")
+        n4_list = load_list(n4, "n4_list")
         gain = keep.tile([P, PACK], F32, name="gain")
         nc.sync.dma_start(gain[:], gs.rearrange("(p t) o -> p (t o)", t=PACK))
-        n5_l = load_list(n5, "n5_l")
+        n5_list = load_list(n5, "n5_list")
         mem_dealt = mem.rearrange("(p t) u -> t p u", t=PACK)
         out_dealt = out.rearrange("(p t) u -> t p u", t=PACK)
         page = [tile_of("page%d" % t, U, F32) for t in range(PACK)]
         for t in range(PACK):
             nc.sync.dma_start(page[t][:], mem_dealt[t])
 
-        def pick(table, offsets, name, dtype, tag=""):
-            picked = tile_of(name, S, dtype, tag)
+        def pick(table, offsets, name, dtype, reuse=""):
+            picked = tile_of(name, S, dtype, reuse)
             nc.vector.tensor_copy(picked[:], table[:].indirect(offsets[:]))
             return picked
 
-        def round_weights(raw, name, tag=""):
-            rounded = tile_of(name, PACK * K, BF16, tag)
+        def round_weights(pieces, name):
+            rounded = tile_of(name, PACK * K, BF16)
             dealt = rounded[:].rearrange("p (t m j) -> p m t j", t=PACK, j=PACK)
-            for part, cols in raw:
+            for raw, cols in pieces:
                 nc.scalar.activation(
                     dealt[:, cols[0] // PACK : cols[1] // PACK],
-                    part[:].rearrange("p j (m t) -> p m t j", t=PACK),
+                    raw[:].rearrange("p j (m t) -> p m t j", t=PACK),
                     ACT.Copy,
                 )
             return rounded
 
-        def quantise(rounded, cols, name, tag=""):
-            codes = tile_of(name + "_codes", cols, U32, tag)
+        def quantise(rounded, cols, name, reuse=""):
+            codes = tile_of(name + "_codes", cols, U32, reuse)
             scales = tile_of(name + "_scales", cols, U8)
             nc.vector.quantize_mx(out=codes[:].bitcast(FP8X4), scales=scales[:], in_=rounded[:])
             return codes, scales
@@ -115,180 +119,175 @@ def tile_picked_twcpathbpaget_none_p_kernel(
             )
             return acc
 
-        offs_scales = pick(table_scales, offs_l, "offs_scales", U8)
-        two_scales = pick(table_scales, two_l, "two_scales", U8)
-        cand_scales = pick(table_scales, cand_l, "cand_scales", U8)
-        offs_words = pick(table_words, offs_l, "offs_words", U32)
-        cand_words = pick(table_words, cand_l, "cand_words", U32)
-        w1_q = quantise(round_weights(w1_raw, "w1_bf16"), K, "w1")
-        two_words = pick(table_words, two_l, "two_words", U32, "w1_raw1")
-        y_acc = [product(t, S, w1_q, t, (offs_words, offs_scales)) for t in range(PACK)]
+        offs_scales = pick(table_scales, offs_list, "offs_scales", U8)
+        two_scales = pick(table_scales, two_list, "two_scales", U8)
+        cand_scales_listed = pick(table_scales, cand_list, "cand_scales_listed", U8)
+        offs_words = pick(table_words, offs_list, "offs_words", U32)
+        cand_words = tile_of("cand_words", S, U32)
+        nc.vector.tensor_copy(
+            cand_words[:].rearrange("p (t m) -> p m t", t=PACK), table_words[:].indirect(cand_list[:])
+        )
+        w1_mx = quantise(round_weights(w1_raw, "w1_bf16"), K, "w1")
+        two_words = pick(table_words, two_list, "two_words", U32, reuse="w1_raw1")
+        y_acc = [product(t, S, w1_mx, t, (offs_words, offs_scales)) for t in range(PACK)]
+
         y_rows = [tile_of("y_rows%d" % t, 2 * S, F32) for t in range(2)]
         nc.scalar.copy(y_rows[0][:, :S], y_acc[0][:])
         nc.scalar.copy(y_rows[1][:, :S], y_acc[1][:])
         w2_bf16 = round_weights(w2_raw, "w2_bf16")
-        y_rows.append(tile_of("y_rows2", 2 * S, F32, "w2_raw1"))
+        y_rows.append(tile_of("y_rows2", 2 * S, F32, reuse="w2_raw1"))
         y_rows.append(tile_of("y_rows3", 2 * S, F32))
         nc.scalar.copy(y_rows[2][:, :S], y_acc[2][:])
         nc.scalar.copy(y_rows[3][:, :S], y_acc[3][:])
 
-        def deal(picked, name, dtype, tag):
-            dealt = tile_of(name, S, dtype, tag)
-            nc.vector.tensor_copy(
-                dealt[:].rearrange("p (t m) -> p t m", t=PACK),
-                picked[:].rearrange("p (m t) -> p t m", t=PACK),
-            )
-            return dealt
+        cand_scales = tile_of("cand_scales", S, U8, reuse="w1_bf16")
+        nc.vector.tensor_copy(
+            cand_scales[:].rearrange("p (t m) -> p t m", t=PACK),
+            cand_scales_listed[:].rearrange("p (m t) -> p t m", t=PACK),
+        )
+        cand_mx = (cand_words, cand_scales)
 
-        cand_scales_dealt = deal(cand_scales, "cand_scales_dealt", U8, "w1_bf16")
-        whole = (0, S)
-        first = (0, HALF)
-        second = (HALF, S)
+        made = {}
 
-        def entries(lst, part):
-            return lst[:, part[0] // 16 : part[1] // 16]
+        def make(name, t, part, reuse=""):
+            label = "%s_%d_%d" % (name, t, part[0])
+            made[(name, t, part)] = tile_of(label, part[1] - part[0], F32, reuse)
+            return made[(name, t, part)][:]
 
-        held = {}
+        def view(name, t, part):
+            if (name, t, part) in made:
+                return made[(name, t, part)][:]
+            return made[(name, t, WHOLE)][:, part[0] : part[1]]
 
-        def fetch(name, t, part, lst, tag):
-            got = tile_of("%s_%d_%d" % (name, t, part[0]), part[1] - part[0], F32, tag)
-            nc.vector.tensor_copy(got[:], y_rows[t][:].indirect(entries(lst, part)))
-            held[(name, t, part)] = got
+        def entries(offsets, part):
+            return offsets[:, part[0] // GROUP : part[1] // GROUP]
 
-        def fetch_add(name, other, t, part, lst, tag):
-            got = tile_of("%s_%d_%d" % (name, t, part[0]), part[1] - part[0], F32, tag)
-            if (other, t, part) in held:
-                addend = held[(other, t, part)][:]
-            else:
-                addend = held[(other, t, whole)][:, part[0] : part[1]]
-            nc.vector.tensor_tensor(got[:], d_rows[t][:].indirect(entries(lst, part)), addend, ALU.add)
-            held[(name, t, part)] = got
+        def y_at_n1(t, part, reuse=""):
+            nc.vector.tensor_copy(make("y1", t, part, reuse), y_rows[t][:].indirect(entries(n1_list, part)))
 
-        z_bf16 = {h: tile_of("z_bf16_%d" % h[0], HALF * PACK, BF16) for h in (first, second)}
+        def y_at_n2(t, part, reuse=""):
+            nc.vector.tensor_copy(make("y2", t, part, reuse), y_rows[t][:].indirect(entries(n2_list, part)))
+
+        def sum_a(t, part, reuse=""):
+            looked_up = d_rows[t][:].indirect(entries(n3_list, part))
+            nc.vector.tensor_tensor(make("a", t, part, reuse), looked_up, view("y1", t, part), ALU.add)
+
+        def sum_b(t, part, reuse=""):
+            looked_up = d_rows[t][:].indirect(entries(n4_list, part))
+            nc.vector.tensor_tensor(make("b", t, part, reuse), looked_up, view("y2", t, part), ALU.add)
+
+        z_bf16 = {half: tile_of("z_bf16_%d" % half[0], HALF * PACK, BF16) for half in (FIRST, SECOND)}
 
         def larger(t, part):
-            got = tile_of("m_%d_%d" % (t, part[0]), part[1] - part[0], F32)
-            nc.vector.tensor_tensor(got[:], held[("a", t, part)][:], held[("b", t, part)][:], ALU.max)
-            for h in (first, second):
-                if part[0] <= h[0] and h[1] <= part[1]:
-                    nc.scalar.activation(
-                        z_bf16[h][:].rearrange("p (c t) -> p c t", t=PACK)[:, :, t],
-                        got[:, h[0] - part[0] : h[1] - part[0]],
-                        ACT.Copy,
-                        scale=gain[:, t : t + 1],
-                    )
+            nc.vector.tensor_tensor(make("max", t, part), view("a", t, part), view("b", t, part), ALU.max)
+            for half in (FIRST, SECOND) if part == WHOLE else (part,):
+                nc.scalar.activation(
+                    z_bf16[half][:].rearrange("p (c t) -> p c t", t=PACK)[:, :, t],
+                    view("max", t, half),
+                    ACT.Copy,
+                    scale=gain[:, t : t + 1],
+                )
 
-        def u1(t, part, tag=""):
-            fetch("u1", t, part, n1_l, tag)
+        def blend_view(name, t, part, reuse=""):
+            span = part if t < 2 else WHOLE
+            if (name, t, span) not in made:
+                make(name, t, span, reuse)
+            return view(name, t, part)
 
-        def u2(t, part, tag=""):
-            fetch("u2", t, part, n2_l, tag)
+        score_acc = {}
 
-        def a(t, part, tag=""):
-            fetch_add("a", "u1", t, part, n3_l, tag)
+        def score(half, z_mx):
+            for t in range(PACK):
+                bank = t if half == FIRST else PACK + t
+                score_acc[(t, half)] = product(bank, HALF, cand_mx, t, z_mx)
 
-        def b(t, part, tag=""):
-            fetch_add("b", "u2", t, part, n4_l, tag)
+        def weight_of_old(t, half):
+            tanh = make("tanh", t, half)
+            nc.scalar.activation(tanh, score_acc[(t, half)][:], ACT.Tanh, scale=SCORE_SCALE / 2)
+            nc.scalar.activation(blend_view("old_weight", t, half), tanh, ACT.Copy, scale=-0.5, bias=0.5)
 
-        def piece(name, t, part, tag=""):
-            span = part if t < 2 else whole
-            if (name, t, span) not in held:
-                held[(name, t, span)] = tile_of("%s_%d_%d" % (name, t, span[0]), span[1] - span[0], F32, tag)
-            return held[(name, t, span)][:, part[0] - span[0] : part[1] - span[0]]
+        def new_term(t, half, reuse=""):
+            nc.scalar.activation(
+                blend_view("new", t, half, reuse), score_acc[(t, half)][:], ACT.Silu, scale=SCORE_SCALE
+            )
 
-        s_acc = {}
-
-        def score(t, part, cand_q, z_q):
-            bank = t + (PACK if part == second else 0)
-            acc = product(bank, HALF, cand_q, t, z_q)
-            s_acc[(t, part)] = acc
-
-        def gates(t, part):
-            th = tile_of("th_%d_%d" % (t, part[0]), HALF, F32)
-            nc.scalar.activation(th[:], s_acc[(t, part)][:], ACT.Tanh, scale=0.03125)
-            nc.scalar.activation(piece("keep_old", t, part), th[:], ACT.Copy, scale=-0.5, bias=0.5)
-
-        def gated(t, part, tag=""):
-            nc.scalar.activation(piece("gated", t, part, tag), s_acc[(t, part)][:], ACT.Silu, scale=0.0625)
-
-        def fetch_old(t, part):
+        def old_term(t, part):
             nc.vector.tensor_tensor(
-                piece("kept", t, part),
-                page[t][:].indirect(entries(n5_l, part)),
-                piece("keep_old", t, part),
+                blend_view("old", t, part),
+                page[t][:].indirect(entries(n5_list, part)),
+                blend_view("old_weight", t, part),
                 ALU.mult,
             )
 
-        def put(t, part):
+        def put_back(t, part):
             nc.vector.tensor_tensor(
-                page[t][:].indirect(entries(n5_l, part)),
-                piece("kept", t, part),
-                piece("gated", t, part),
+                page[t][:].indirect(entries(n5_list, part)),
+                blend_view("old", t, part),
+                blend_view("new", t, part),
                 ALU.add,
             )
             if part[1] == S:
                 nc.sync.dma_start(out_dealt[t], page[t][:])
 
-        u1(0, whole)
-        u2(0, whole)
-        u1(1, whole)
-        u2(1, whole)
-        w2_q = quantise(w2_bf16, K, "w2")
-        for t in range(PACK):
-            d_acc = product(PACK + t, S, w2_q, t, (two_words, two_scales))
-            nc.scalar.copy(d_rows[t][:, :S], d_acc[:])
-        u1(2, whole)
-        u2(2, whole)
-        a(0, whole)
-        b(0, whole)
-        a(1, whole)
-        larger(0, whole)
-        b(1, whole)
-        a(2, first)
-        larger(1, whole)
-        b(2, first)
-        u1(3, first, "u1_1_0")
-        larger(2, first)
-        u2(3, first, "u2_1_0")
-        a(3, first)
-        b(3, first)
-        u1(3, second, "u1_1_0")
-        larger(3, first)
-        u2(3, second, "u2_1_0")
-        cand_q = (deal(cand_words, "cand_words_dealt", U32, "a_1_0"), cand_scales_dealt)
-        a(2, second, "a_3_0")
-        z_first = quantise(z_bf16[first], HALF, "z_first")
-        for t in range(PACK):
-            score(t, first, cand_q, z_first)
         for t in range(2):
-            gates(t, first)
-        gated(0, first)
-        a(3, second, "b_3_0")
-        b(2, second, "z_bf16_0")
-        b(3, second, "m_3_0")
-        larger(2, second)
-        larger(3, second)
-        gated(1, first, "m_3_256")
+            y_at_n1(t, WHOLE)
+            y_at_n2(t, WHOLE)
+        w2_mx = quantise(w2_bf16, K, "w2")
+        for t in range(PACK):
+            d_acc = product(PACK + t, S, w2_mx, t, (two_words, two_scales))
+            nc.scalar.copy(d_rows[t][:, :S], d_acc[:])
+        y_at_n1(2, WHOLE)
+        y_at_n2(2, WHOLE)
+
+        sum_a(0, WHOLE)
+        sum_b(0, WHOLE)
+        sum_a(1, WHOLE)
+        larger(0, WHOLE)
+        sum_b(1, WHOLE)
+        sum_a(2, FIRST)
+        larger(1, WHOLE)
+        sum_b(2, FIRST)
+        y_at_n1(3, FIRST, reuse="y1_1_0")
+        larger(2, FIRST)
+        y_at_n2(3, FIRST, reuse="y2_1_0")
+        sum_a(3, FIRST)
+        sum_b(3, FIRST)
+        y_at_n1(3, SECOND, reuse="y1_1_0")
+        larger(3, FIRST)
+
+        y_at_n2(3, SECOND, reuse="y2_1_0")
+        sum_a(2, SECOND, reuse="a_3_0")
+        score(FIRST, quantise(z_bf16[FIRST], HALF, "z_first"))
+        weight_of_old(0, FIRST)
+        weight_of_old(1, FIRST)
+        new_term(0, FIRST)
+        sum_a(3, SECOND, reuse="b_3_0")
+        sum_b(2, SECOND, reuse="z_bf16_0")
+        sum_b(3, SECOND, reuse="max_3_0")
+        larger(2, SECOND)
+        larger(3, SECOND)
+        new_term(1, FIRST, reuse="max_3_256")
+        weight_of_old(2, FIRST)
+        weight_of_old(3, FIRST)
+
+        old_term(0, FIRST)
+        old_term(1, FIRST)
+        put_back(0, FIRST)
+        z_second = quantise(z_bf16[SECOND], HALF, "z_second", reuse="old_weight_1_0")
+        put_back(1, FIRST)
+        old_term(2, FIRST)
+        score(SECOND, z_second)
+        for t in range(PACK):
+            weight_of_old(t, SECOND)
+        new_term(0, SECOND)
+        new_term(1, SECOND)
         for t in range(2, PACK):
-            gates(t, first)
-        fetch_old(0, first)
-        fetch_old(1, first)
-        put(0, first)
-        z_second = quantise(z_bf16[second], HALF, "z_second", "keep_old_1_0")
-        put(1, first)
-        fetch_old(2, first)
-        for t in range(PACK):
-            score(t, second, cand_q, z_second)
-        for t in range(PACK):
-            gates(t, second)
-        for t in range(PACK):
-            if t >= 2:
-                gated(t, first)
-            gated(t, second)
+            new_term(t, FIRST)
+            new_term(t, SECOND)
         for t in range(PACK - 1):
-            fetch_old(t, second)
-        fetch_old(3, whole)
-        put(0, second)
-        put(1, second)
-        put(2, whole)
-        put(3, whole)
+            old_term(t, SECOND)
+        old_term(3, WHOLE)
+        put_back(0, SECOND)
+        put_back(1, SECOND)
+        put_back(2, WHOLE)
+        put_back(3, WHOLE)

from contextlib import ExitStack

import concourse.mybir as mybir

F32 = mybir.dt.float32
BF16 = mybir.dt.bfloat16
I32 = mybir.dt.int32
U32 = mybir.dt.uint32
U16 = mybir.dt.uint16
U8 = mybir.dt.uint8
FP8X4 = mybir.dt.float8_e4m3fn_x4
ALU = mybir.AluOpType
ACT = mybir.ActivationFunctionType

P = 128
PACK = 4
GROUP = 16
BLOCK = 32
QUADRANT = 32
SCALE_ROWS = QUADRANT * PACK // BLOCK
K, T, S, U = 512, 2048, 512, 1024
HALF = S // 2
WHOLE, FIRST, SECOND = (0, S), (0, HALF), (HALF, S)
SCORE_SCALE = 0.0625
W1_SPLIT = 320
FLOPS = 3 * 2 * 512 * 512 * 512


def tile_picked_twcpathbpaget_none_p_kernel(
    tc, x_words, x_scales, w1, w2, gs, mem, offs, two, n1, n2, n3, n4, cand, n5, out
):
    nc = tc.nc
    with ExitStack() as ctx:
        keep = ctx.enter_context(tc.tile_pool(name="keep", bufs=1))
        psum = ctx.enter_context(tc.psum_pool(name="psum", bufs=1))

        def tile_of(name, cols, dtype, reuse=""):
            return keep.tile([P, cols], dtype, name=name, tag=reuse or name, align_bytes=64)

        def load_list(src, name):
            offsets = keep.tile([P, S // GROUP], U16, name=name)
            nc.sync.dma_start(offsets[:], src)
            return offsets

        def load_weights(w, name, cols):
            raw = keep.tile([P, PACK, cols[1] - cols[0]], F32, name=name, align_bytes=64)
            nc.sync.dma_start(raw[:], w.rearrange("(p j) c -> p j c", j=PACK)[:, :, cols[0] : cols[1]])
            return raw, cols

        table_scales = tile_of("table_scales", T, U8)
        nc.vector.memset(table_scales[:].bitcast(I32), 0)
        d_rows = [tile_of("d_rows%d" % t, 2 * S, F32) for t in range(PACK)]
        warm_in = keep.tile([P, 1], F32, name="warm_in")
        warm_out = keep.tile([P, 1], F32, name="warm_out")
        nc.gpsimd.memset(warm_in[:], 0.0)

        offs_list = load_list(offs, "offs_list")
        for r in range(SCALE_ROWS):
            nc.sync.dma_start(
                table_scales[r:P:QUADRANT, :].bitcast(I32),
                x_scales[0, r : K // BLOCK : SCALE_ROWS, :].bitcast(I32),
            )
        nc.scalar.activation(warm_out[:], warm_in[:], ACT.Silu)
        two_list = load_list(two, "two_list")
        cand_list = load_list(cand, "cand_list")
        w1_raw = [load_weights(w1, "w1_raw0", (0, W1_SPLIT))]
        table_words = tile_of("table_words", T, U32)
        nc.sync.dma_start(
            table_words[:].bitcast(I32), x_words[0].rearrange("p c r -> p (c r)").bitcast(I32)
        )
        w1_raw.append(load_weights(w1, "w1_raw1", (W1_SPLIT, K)))
        w2_raw = [load_weights(w2, "w2_raw0", (0, K // 2)), load_weights(w2, "w2_raw1", (K // 2, K))]
        n1_list = load_list(n1, "n1_list")
        n2_list = load_list(n2, "n2_list")
        n3_list = load_list(n3, "n3_list")
        n4_list = load_list(n4, "n4_list")
        gain = keep.tile([P, PACK], F32, name="gain")
        nc.sync.dma_start(gain[:], gs.rearrange("(p t) o -> p (t o)", t=PACK))
        n5_list = load_list(n5, "n5_list")
        mem_dealt = mem.rearrange("(p t) u -> t p u", t=PACK)
        out_dealt = out.rearrange("(p t) u -> t p u", t=PACK)
        page = [tile_of("page%d" % t, U, F32) for t in range(PACK)]
        for t in range(PACK):
            nc.sync.dma_start(page[t][:], mem_dealt[t])

        def pick(table, offsets, name, dtype, reuse=""):
            picked = tile_of(name, S, dtype, reuse)
            nc.vector.tensor_copy(picked[:], table[:].indirect(offsets[:]))
            return picked

        def round_weights(pieces, name):
            rounded = tile_of(name, PACK * K, BF16)
            dealt = rounded[:].rearrange("p (t m j) -> p m t j", t=PACK, j=PACK)
            for raw, cols in pieces:
                nc.scalar.activation(
                    dealt[:, cols[0] // PACK : cols[1] // PACK],
                    raw[:].rearrange("p j (m t) -> p m t j", t=PACK),
                    ACT.Copy,
                )
            return rounded

        def quantise(rounded, cols, name, reuse=""):
            codes = tile_of(name + "_codes", cols, U32, reuse)
            scales = tile_of(name + "_scales", cols, U8)
            nc.vector.quantize_mx(out=codes[:].bitcast(FP8X4), scales=scales[:], in_=rounded[:])
            return codes, scales

        def product(bank, cols, stationary, t, moving):
            acc = psum.tile([P, cols], F32, name="acc", tag="bank%d" % bank)
            rows = slice(t * P, (t + 1) * P)
            nc.tensor.matmul_mx(
                out=acc[:],
                lhsT=stationary[0][:, rows].bitcast(FP8X4),
                lhsT_scale=stationary[1][:, rows],
                rhs=moving[0][:].bitcast(FP8X4),
                rhs_scale=moving[1][:],
                start=True,
                stop=True,
            )
            return acc

        offs_scales = pick(table_scales, offs_list, "offs_scales", U8)
        two_scales = pick(table_scales, two_list, "two_scales", U8)
        cand_scales_listed = pick(table_scales, cand_list, "cand_scales_listed", U8)
        offs_words = pick(table_words, offs_list, "offs_words", U32)
        cand_words = tile_of("cand_words", S, U32)
        nc.vector.tensor_copy(
            cand_words[:].rearrange("p (t m) -> p m t", t=PACK), table_words[:].indirect(cand_list[:])
        )
        w1_mx = quantise(round_weights(w1_raw, "w1_bf16"), K, "w1")
        two_words = pick(table_words, two_list, "two_words", U32, reuse="w1_raw1")
        y_acc = [product(t, S, w1_mx, t, (offs_words, offs_scales)) for t in range(PACK)]

        y_rows = [tile_of("y_rows%d" % t, 2 * S, F32) for t in range(2)]
        nc.scalar.copy(y_rows[0][:, :S], y_acc[0][:])
        nc.scalar.copy(y_rows[1][:, :S], y_acc[1][:])
        w2_bf16 = round_weights(w2_raw, "w2_bf16")
        y_rows.append(tile_of("y_rows2", 2 * S, F32, reuse="w2_raw1"))
        y_rows.append(tile_of("y_rows3", 2 * S, F32))
        nc.scalar.copy(y_rows[2][:, :S], y_acc[2][:])
        nc.scalar.copy(y_rows[3][:, :S], y_acc[3][:])

        cand_scales = tile_of("cand_scales", S, U8, reuse="w1_bf16")
        nc.vector.tensor_copy(
            cand_scales[:].rearrange("p (t m) -> p t m", t=PACK),
            cand_scales_listed[:].rearrange("p (m t) -> p t m", t=PACK),
        )
        cand_mx = (cand_words, cand_scales)

        made = {}

        def make(name, t, part, reuse=""):
            label = "%s_%d_%d" % (name, t, part[0])
            made[(name, t, part)] = tile_of(label, part[1] - part[0], F32, reuse)
            return made[(name, t, part)][:]

        def view(name, t, part):
            if (name, t, part) in made:
                return made[(name, t, part)][:]
            return made[(name, t, WHOLE)][:, part[0] : part[1]]

        def entries(offsets, part):
            return offsets[:, part[0] // GROUP : part[1] // GROUP]

        def y_at_n1(t, part, reuse=""):
            nc.vector.tensor_copy(make("y1", t, part, reuse), y_rows[t][:].indirect(entries(n1_list, part)))

        def y_at_n2(t, part, reuse=""):
            nc.vector.tensor_copy(make("y2", t, part, reuse), y_rows[t][:].indirect(entries(n2_list, part)))

        def sum_a(t, part, reuse=""):
            looked_up = d_rows[t][:].indirect(entries(n3_list, part))
            nc.vector.tensor_tensor(make("a", t, part, reuse), looked_up, view("y1", t, part), ALU.add)

        def sum_b(t, part, reuse=""):
            looked_up = d_rows[t][:].indirect(entries(n4_list, part))
            nc.vector.tensor_tensor(make("b", t, part, reuse), looked_up, view("y2", t, part), ALU.add)

        z_bf16 = {half: tile_of("z_bf16_%d" % half[0], HALF * PACK, BF16) for half in (FIRST, SECOND)}

        def larger(t, part):
            nc.vector.tensor_tensor(make("max", t, part), view("a", t, part), view("b", t, part), ALU.max)
            for half in (FIRST, SECOND) if part == WHOLE else (part,):
                nc.scalar.activation(
                    z_bf16[half][:].rearrange("p (c t) -> p c t", t=PACK)[:, :, t],
                    view("max", t, half),
                    ACT.Copy,
                    scale=gain[:, t : t + 1],
                )

        def blend_view(name, t, part, reuse=""):
            span = part if t < 2 else WHOLE
            if (name, t, span) not in made:
                make(name, t, span, reuse)
            return view(name, t, part)

        score_acc = {}

        def score(half, z_mx):
            for t in range(PACK):
                bank = t if half == FIRST else PACK + t
                score_acc[(t, half)] = product(bank, HALF, cand_mx, t, z_mx)

        def weight_of_old(t, half):
            tanh = make("tanh", t, half)
            nc.scalar.activation(tanh, score_acc[(t, half)][:], ACT.Tanh, scale=SCORE_SCALE / 2)
            nc.scalar.activation(blend_view("old_weight", t, half), tanh, ACT.Copy, scale=-0.5, bias=0.5)

        def new_term(t, half, reuse=""):
            nc.scalar.activation(
                blend_view("new", t, half, reuse), score_acc[(t, half)][:], ACT.Silu, scale=SCORE_SCALE
            )

        def old_term(t, part):
            nc.vector.tensor_tensor(
                blend_view("old", t, part),
                page[t][:].indirect(entries(n5_list, part)),
                blend_view("old_weight", t, part),
                ALU.mult,
            )

        def put_back(t, part):
            nc.vector.tensor_tensor(
                page[t][:].indirect(entries(n5_list, part)),
                blend_view("old", t, part),
                blend_view("new", t, part),
                ALU.add,
            )
            if part[1] == S:
                nc.sync.dma_start(out_dealt[t], page[t][:])

        for t in range(2):
            y_at_n1(t, WHOLE)
            y_at_n2(t, WHOLE)
        w2_mx = quantise(w2_bf16, K, "w2")
        for t in range(PACK):
            d_acc = product(PACK + t, S, w2_mx, t, (two_words, two_scales))
            nc.scalar.copy(d_rows[t][:, :S], d_acc[:])
        y_at_n1(2, WHOLE)
        y_at_n2(2, WHOLE)

        sum_a(0, WHOLE)
        sum_b(0, WHOLE)
        sum_a(1, WHOLE)
        larger(0, WHOLE)
        sum_b(1, WHOLE)
        sum_a(2, FIRST)
        larger(1, WHOLE)
        sum_b(2, FIRST)
        y_at_n1(3, FIRST, reuse="y1_1_0")
        larger(2, FIRST)
        y_at_n2(3, FIRST, reuse="y2_1_0")
        sum_a(3, FIRST)
        sum_b(3, FIRST)
        y_at_n1(3, SECOND, reuse="y1_1_0")
        larger(3, FIRST)

        y_at_n2(3, SECOND, reuse="y2_1_0")
        sum_a(2, SECOND, reuse="a_3_0")
        score(FIRST, quantise(z_bf16[FIRST], HALF, "z_first"))
        weight_of_old(0, FIRST)
        weight_of_old(1, FIRST)
        new_term(0, FIRST)
        sum_a(3, SECOND, reuse="b_3_0")
        sum_b(2, SECOND, reuse="z_bf16_0")
        sum_b(3, SECOND, reuse="max_3_0")
        larger(2, SECOND)
        larger(3, SECOND)
        new_term(1, FIRST, reuse="max_3_256")
        weight_of_old(2, FIRST)
        weight_of_old(3, FIRST)

        old_term(0, FIRST)
        old_term(1, FIRST)
        put_back(0, FIRST)
        z_second = quantise(z_bf16[SECOND], HALF, "z_second", reuse="old_weight_1_0")
        put_back(1, FIRST)
        old_term(2, FIRST)
        score(SECOND, z_second)
        for t in range(PACK):
            weight_of_old(t, SECOND)
        new_term(0, SECOND)
        new_term(1, SECOND)
        for t in range(2, PACK):
            new_term(t, FIRST)
            new_term(t, SECOND)
        for t in range(PACK - 1):
            old_term(t, SECOND)
        old_term(3, WHOLE)
        put_back(0, SECOND)
        put_back(1, SECOND)
        put_back(2, WHOLE)
        put_back(3, WHOLE)
